import numpy as np
import ml_dtypes


def mxq(x, axis, fmt="e4m3"):
    dtype, down = {"e4m3": (ml_dtypes.float8_e4m3fn, 7), "e5m2": (ml_dtypes.float8_e5m2, 14)}[fmt]
    v = np.moveaxis(np.asarray(x, np.float32).astype(ml_dtypes.bfloat16).astype(np.float64), axis, -1)
    blocks = v.reshape(v.shape[:-1] + (-1, 32))
    amax = np.abs(blocks).max(-1, keepdims=True)
    byte = np.maximum(np.where(amax > 0, np.frexp(amax)[1] - 1 + 127, 0) - down, 1)
    scale = np.exp2(byte - 127.0)
    codes = (blocks / scale).astype(np.float32).astype(dtype).astype(np.float64)
    return np.moveaxis((codes * scale).reshape(v.shape), -1, axis)


WIDE = False


def mx_kscale(k):
    if not WIDE:
        return np.ones(k)
    levels = np.array([10, -10, 5, -5, 0])
    if k % 512:
        return np.exp2(np.random.permutation(np.resize(levels, k // 32))).repeat(32)
    a = np.empty((k // 512, 16))
    for p in range(k // 512):
        a[p, :8] = np.random.permutation(np.resize(levels, 8))
        for g in range(8):
            far = levels[np.abs(levels - a[p, g]) >= 10]
            a[p, g + 8] = far[np.random.randint(len(far))]
    return np.exp2(a.ravel()).repeat(32)


def f64(x):
    return np.asarray(x).astype(np.float64)


def striped(idx):
    return np.tile(np.asarray(idx).reshape(-1, 16).T, (8, 1)).astype(np.uint16)


def unstriped(offs):
    return offs[:16].T.reshape(-1).astype(np.int64)


E2M1 = np.array([0.0, 0.5, 1.0, 1.5, 2.0, 3.0, 4.0, 6.0, -0.0, -0.5, -1.0, -1.5, -2.0, -3.0, -4.0, -6.0])


def pack_weight(w, fmt):
    k, n = w.shape
    w = f64(np.asarray(w, np.float32).astype(ml_dtypes.bfloat16)).reshape(k // 32, 32, n)
    amax = np.abs(w).max(1)
    if fmt == "e4m3":
        byte = np.frexp(amax)[1] - 1 + 127 - 7
    else:
        mant, ex = np.frexp(amax / 6.0)
        byte = np.where(mant > 0.5, ex, ex - 1) + 127
    byte = np.clip(np.where(amax > 0, byte, 1), 1, 254)
    scaled = (w * np.exp2(127.0 - byte)[:, None, :]).reshape(k, n).astype(np.float32)
    by_word = np.ascontiguousarray(scaled.reshape(k // 512, 128, 4, n).transpose(0, 1, 3, 2))
    if fmt == "e4m3":
        words = by_word.astype(ml_dtypes.float8_e4m3fn).view(np.uint8)
    else:
        c = by_word.astype(ml_dtypes.float4_e2m1fn).view(np.uint8) & 0xF
        words = (c[..., 0::2] | (c[..., 1::2] << 4)).reshape(k // 512, 128, 2 * n)
    return np.ascontiguousarray(words), np.ascontiguousarray(byte.astype(np.uint8).reshape(k // 512, 16, n))


def unpack_weight(words, scales, fmt):
    g, _, n = scales.shape
    words = np.ascontiguousarray(words).reshape(g, 128, n, -1)
    if fmt == "e4m3":
        vals = words.view(ml_dtypes.float8_e4m3fn).astype(np.float64)
    else:
        nib = np.empty((g, 128, n, 4), np.uint8)
        nib[..., 0::2] = words & 0xF
        nib[..., 1::2] = words >> 4
        vals = E2M1[nib]
    vals = vals * np.repeat(np.exp2(scales.astype(np.float64) - 127.0), 8, axis=1)[..., None]
    return vals.transpose(0, 1, 3, 2).reshape(g * 512, n)


B, N, T, D, DV, NQ = 1, 2048, 4096, 512, 128, 128
PAGE = 512


def setup_inputs():
    n = np.random.standard_normal
    pages = np.random.permutation(T // PAGE)[:B * N // PAGE]
    idx = (pages[:, None] * PAGE + np.arange(PAGE)[None, :]).reshape(-1)
    s = mx_kscale(D)[:, None]
    u = np.ones(T)
    u[idx] = mx_kscale(B * N)
    r = np.random.uniform(0.5, 2.0, T)
    k = n((D, T)) / s
    v = n((DV, T)) / (u * r)
    kp = pack_weight(k, "e4m3")
    vp = pack_weight(v.T, "e4m3")
    return {
        "qT": (n((B, D, NQ)) * s * (0.80 / np.sqrt(D))).astype(np.float32),
        "k_words": kp[0],
        "k_scales": kp[1],
        "v_words": vp[0],
        "v_scales": vp[1],
        "vs": np.tile(u * r, (128, 1)).astype(np.float32),
        "og": n((B, NQ, DV)).astype(np.float32),
        "offs": striped(idx),
        "voffs": striped((pages[:, None] * DV + np.arange(DV)[None, :]).reshape(-1)),
    }


def reference(qT, k_words, k_scales, v_words, v_scales, vs, og, offs, voffs):
    idx = unstriped(offs)
    k = unpack_weight(k_words, k_scales, "e4m3")
    v = unpack_weight(v_words, v_scales, "e4m3")
    v = v.reshape(T // 512, 512, DV)[unstriped(voffs)[::DV] // DV].reshape(B, N, DV)
    pick = lambda x: x[:, idx].reshape(x.shape[0], B, N).transpose(1, 0, 2)
    q = f64(qT)
    score = mxq(q, 1, "e4m3").transpose(0, 2, 1) @ pick(k)
    p = 1.0 / (1.0 + np.exp(-score))
    w = p * pick(f64(vs))[:, :1, :]
    y = mxq(w, 2, "e4m3") @ v
    y = y / 16.0
    y = y / (1.0 + np.exp(-f64(og)))
    return y

from contextlib import ExitStack

import concourse.mybir as mybir
from concourse.masks import make_identity

N, T, D, DV, NQ = 2048, 4096, 512, 128, 128
P = 128
PACK = 4
PAGE = P * PACK
PAGES = N // PAGE
POOL_PAGES = T // PAGE
SCALAR_PAGES = 2
FLOPS = 2 * NQ * N * (D + DV)
BYTES = T * D + T * D // 32 + T * DV + T * DV // 32 + 4 * (T + D * NQ + 2 * NQ * DV) + 2 * P * (N + PAGES * DV) // 16

F32 = mybir.dt.float32
BF16 = mybir.dt.bfloat16
I32 = mybir.dt.int32
U32 = mybir.dt.uint32
U16 = mybir.dt.uint16
U8 = mybir.dt.uint8
FP8X4 = mybir.dt.float8_e4m3fn_x4
ACT = mybir.ActivationFunctionType
MULT = mybir.AluOpType.mult


def tile_attend_pkv8_sigm_gate_kernel(tc, qT, k_words, k_scales, v_words, v_scales, vs, og, offs, voffs, out):
    nc = tc.nc
    with ExitStack() as ctx:
        keep = ctx.enter_context(tc.tile_pool(name="keep", bufs=1))
        psum = ctx.enter_context(tc.psum_pool(name="psum", bufs=1))

        offs_t = keep.tile([P, N // 16], U16, name="offs_t")
        voffs_t = keep.tile([P, PAGES * DV // 16], U16, name="voffs_t")
        og_t = keep.tile([P, DV], F32, name="og_t")
        q_raw = keep.tile([P, PACK, NQ], F32, name="q_raw")
        ks_pool = keep.tile([P, T], U8, name="ks_pool", align_bytes=64)
        kw_pool = keep.tile([P, T], U32, name="kw_pool", align_bytes=64)
        vs_pool = keep.tile([P, T], F32, name="vs_pool", align_bytes=64)
        vw_pool = keep.tile([P, POOL_PAGES * DV], U32, name="vw_pool", align_bytes=64)
        vb_pool = keep.tile([P, POOL_PAGES * DV], U8, name="vb_pool", align_bytes=64)
        ident = keep.tile([P, P], F32, name="ident")

        nc.vector.memset(ks_pool[:].bitcast(I32), 0)
        nc.vector.memset(vs_pool[:].bitcast(I32), 0)
        nc.vector.memset(vb_pool[:].bitcast(I32), 0)
        make_identity(nc, ident[:])

        nc.sync.dma_start(offs_t[:], offs)
        nc.scalar.dma_start(out=q_raw[:], in_=qT[0].rearrange("(p j) q -> p j q", j=PACK))
        nc.sync.dma_start(voffs_t[:], voffs)
        nc.sync.dma_start(out=og_t[:], in_=og[0])
        for quad in range(4):
            nc.sync.dma_start(out=ks_pool[32 * quad : 32 * quad + 4, :].bitcast(I32), in_=k_scales[0, 4 * quad : 4 * quad + 4, :].bitcast(I32))
        nc.sync.dma_start(out=kw_pool[:].bitcast(I32), in_=k_words[0].rearrange("p t r -> p (t r)").bitcast(I32))
        nc.scalar.dma_start(out=vs_pool[0:1, :], in_=vs[0:1, :])
        nc.sync.dma_start(
            out=vw_pool[:].bitcast(I32).rearrange("p (u e) -> p u e", u=POOL_PAGES),
            in_=v_words.rearrange("u p e r -> p u (e r)").bitcast(I32),
        )
        for quad in range(4):
            nc.sync.dma_start(
                out=vb_pool[32 * quad : 32 * quad + 4, :].bitcast(I32).rearrange("f (u e) -> f u e", u=POOL_PAGES),
                in_=v_scales[:, 4 * quad : 4 * quad + 4, :].rearrange("u f e -> f u e").bitcast(I32),
            )

        gate = keep.tile([P, DV], F32, name="gate")
        nc.scalar.activation(out=gate[:], in_=og_t[:], func=ACT.Sigmoid)

        q_bf = keep.tile([P, NQ, PACK], BF16, name="q_bf", align_bytes=64)
        nc.scalar.copy(out=q_bf[:], in_=q_raw[:].rearrange("p j q -> p q j"))
        q_codes = keep.tile([P, NQ], U32, name="q_codes", align_bytes=64)
        q_scale = keep.tile([P, NQ], U8, name="q_scale", align_bytes=64)
        nc.vector.quantize_mx(out=q_codes[:].bitcast(FP8X4), scales=q_scale[:], in_=q_bf[:].rearrange("p q j -> p (q j)"))

        ks_g = keep.tile([P, N], U8, name="ks_g", tag="scale_stage", align_bytes=64)
        nc.vector.tensor_copy(ks_g[:], ks_pool[:].indirect(offs_t[:]))

        def page_offsets(u):
            return offs_t[:, u * (PAGE // 16) : (u + 1) * (PAGE // 16)]

        vs_cols = {}
        p_turned = {}
        w_bf = {}

        def token_scales(u):
            vs_g = keep.tile([P, PAGE], F32, name="vs_g", tag="stage%d" % u, align_bytes=64)
            nc.vector.tensor_copy(vs_g[:], vs_pool[:].indirect(page_offsets(u)))
            turned = psum.tile([P, PACK, P], F32, name="vs_turned", tag="vs_turned%d" % (u % 2))
            for t in range(PACK):
                nc.tensor.transpose(turned[:, t, :], vs_g[:, t::PACK], ident[:])
            cols = keep.tile([P, PACK], F32, name="vs_col", tag="vs_col%d" % u)
            if u < SCALAR_PAGES:
                nc.scalar.copy(out=cols[:], in_=turned[:, :, 0])
            else:
                nc.vector.tensor_copy(out=cols[:], in_=turned[:, :, 0])
            vs_cols[u] = cols

        def score(u):
            kw_g = keep.tile([P, PAGE], U32, name="kw_g", tag="stage%d" % u, align_bytes=64)
            nc.vector.tensor_copy(kw_g[:], kw_pool[:].indirect(page_offsets(u)))
            scores = psum.tile([P, PAGE], F32, name="scores", tag="scores%d" % (u % 2))
            nc.tensor.matmul_mx(
                out=scores[:],
                lhsT=q_codes[:].bitcast(FP8X4),
                lhsT_scale=q_scale[:],
                rhs=kw_g[:].bitcast(FP8X4),
                rhs_scale=ks_g[:, u * PAGE : (u + 1) * PAGE],
                start=True,
                stop=True,
            )
            p = keep.tile([P, PACK, P], F32, name="p", tag="p%d" % u)
            nc.scalar.activation(out=p[:], in_=scores[:].rearrange("q (s t) -> q t s", t=PACK), func=ACT.Sigmoid)
            turned = psum.tile([P, PACK, NQ], F32, name="p_turned", tag="p_turned%d" % u)
            for t in range(PACK):
                nc.tensor.transpose(turned[:, t, :], p[:, t, :], ident[:])
            p_turned[u] = turned

        def weigh_on_scalar(u):
            planes = keep.tile([P, PACK, NQ], BF16, name="planes", tag="planes%d" % u)
            for t in range(PACK):
                nc.scalar.activation(out=planes[:, t, :], in_=p_turned[u][:, t, :], func=ACT.Copy, scale=vs_cols[u][:, t : t + 1])
            w = keep.tile([P, NQ, PACK], BF16, name="w", tag="w%d" % u, align_bytes=64)
            nc.scalar.copy(out=w[:], in_=planes[:].rearrange("s t q -> s q t"))
            w_bf[u] = w

        def weigh_on_vector(u):
            w = keep.tile([P, NQ, PACK], BF16, name="w", tag="w%d" % u, align_bytes=64)
            nc.vector.tensor_tensor(
                w[:],
                p_turned[u][:].rearrange("s t q -> s q t"),
                vs_cols[u][:].unsqueeze(1).to_broadcast([P, NQ, PACK]),
                MULT,
            )
            w_bf[u] = w

        for u in range(PAGES):
            score(u)
        for u in range(PAGES):
            token_scales(u)
        for u in range(SCALAR_PAGES):
            weigh_on_scalar(u)

        vw_g = keep.tile([P, PAGES * DV], U32, name="vw_g", tag="stage0", align_bytes=64)
        nc.vector.tensor_copy(vw_g[:], vw_pool[:].indirect(voffs_t[:]))
        vb_g = keep.tile([P, PAGES * DV], U8, name="vb_g", tag="scale_stage", align_bytes=64)
        nc.vector.tensor_copy(vb_g[:], vb_pool[:].indirect(voffs_t[:]))

        for u in range(SCALAR_PAGES, PAGES):
            weigh_on_vector(u)

        y = psum.tile([P, DV], F32, name="y", tag="scores0")
        for u in range(PAGES):
            w_codes = keep.tile([P, NQ], U32, name="w_codes", tag="w_codes%d" % u, align_bytes=64)
            w_scale = keep.tile([P, NQ], U8, name="w_scale", tag="w_scale%d" % u, align_bytes=64)
            nc.vector.quantize_mx(out=w_codes[:].bitcast(FP8X4), scales=w_scale[:], in_=w_bf[u][:].rearrange("s q t -> s (q t)"))
            nc.tensor.matmul_mx(
                out=y[:],
                lhsT=w_codes[:].bitcast(FP8X4),
                lhsT_scale=w_scale[:],
                rhs=vw_g[:, u * DV : (u + 1) * DV].bitcast(FP8X4),
                rhs_scale=vb_g[:, u * DV : (u + 1) * DV],
                start=(u == 0),
                stop=(u == PAGES - 1),
            )

        result = keep.tile([P, DV], F32, name="result")
        nc.vector.scalar_tensor_tensor(result[:], y[:], 1.0 / 16.0, gate[:], MULT, MULT)
        nc.sync.dma_start(out=out[0], in_=result[:])
